import numpy as np, ml_dtypes
CORES = [125,127,253,255,381,383,509,511]
N = 8
import mx_ref
NC, G = 128, 2
C = np.float32(0.029)
BF = ml_dtypes.bfloat16
def cut(t, i, w=512):
    return t[:, w * i:w * i + w]
def tile(rs):
    return np.stack(rs, axis=2).reshape(128, -1).astype(BF)
def layer(w, X):
    out = []
    for i in range(G):
        for t in range(len(X)):
            p = mx_ref.matmul(mx_ref.quantize(cut(w, len(X) * i + t)), X[t])
            z = p if t == 0 else z + p
        out.append(z)
    return out
def act(Z):
    return [np.maximum(s * z, 0) * C for z in Z for s in (1, -1)]
def setup_inputs(rng):
    def f(*shape):
        return mx_ref.flush((rng.standard_normal(shape, dtype=np.float32) * np.exp2(rng.integers(-2, 3, shape[:-1] + (1,)))).astype(BF))
    return {"x": f(N, 128, 4 * NC), "w1": f(N, 128, G * 512), "w2": f(N, 128, 512)}
def setup_inputs_blocks(rng):
    d = setup_inputs(rng)
    for k in ("x", "w1", "w2"): d[k] = mx_ref.spread(d[k], rng, 2)
    return d
def setup_inputs_wide(rng):
    d = setup_inputs(rng)
    for k in ("x", "w1", "w2"): d[k] = mx_ref.flush((d[k].astype(np.float32) * np.exp2(rng.integers(-6, 7, (N, 1, 1))).astype(np.float32)).astype(BF))
    return d
def reference(x, w1, w2):
    X = [mx_ref.quantize(x[j]) for j in range(N)]
    y = np.zeros((N, 128, NC), np.float32)
    for c in range(N):
        for r in range(N):
            p = mx_ref.matmul(mx_ref.quantize(w2[r]), mx_ref.quantize(tile(act(layer(w1[r], [X[c]])))))
            y[c] = p if r == 0 else y[c] + p
    return {"y": y}

@@ -1,0 +1,203 @@
+import numpy as np
+from concourse.bass import DstId, RemoteDMATransfer
+from concourse.mybir import dt, AluOpType, ActivationFunctionType
+
+NC = 128
+SLICES = [("o", "o"), ("o", "n"), ("o", "d"), ("m", "n"), ("m", "d"), ("m", "o"), ("n", "e"), ("n", "d")]
+C = float(np.float32(0.029))
+
+SCRATCH = {
+    "xt": ("sbuf", [128, 512], "bfloat16"),
+    "w1t": ("sbuf", [128, 1024], "bfloat16"),
+    "w2t": ("sbuf", [128, 512], "bfloat16"),
+    "oq": ("sbuf", [128, 512], "float8_e4m3fn_x4"), "op": ("sbuf", [128, 512], "uint8"),
+    "mq": ("sbuf", [128, 384], "float8_e4m3fn_x4"), "mp": ("sbuf", [128, 384], "uint8"),
+    "nq": ("sbuf", [128, 384], "float8_e4m3fn_x4"), "np": ("sbuf", [128, 384], "uint8"),
+    "xq": ("sbuf", [128, 384], "float8_e4m3fn_x4"), "xp": ("sbuf", [128, 384], "uint8"),
+    "sn": ("sbuf", [128, 128], "float32"), "sd": ("sbuf", [128, 128], "float32"), "se": ("sbuf", [128, 128], "float32"),
+    "ln": ("sbuf", [128, 128], "float32"), "ld": ("sbuf", [128, 128], "float32"), "le": ("sbuf", [128, 128], "float32"),
+    "acc1": ("sbuf", [128, 128], "float32"), "acc2": ("sbuf", [128, 128], "float32"), "acc3": ("sbuf", [128, 128], "float32"),
+    "za0": ("psum", [128, 512], "float32"), "za1": ("psum", [128, 512], "float32"),
+    "zb0": ("psum", [128, 512], "float32"), "zb1": ("psum", [128, 512], "float32"),
+    "yo": ("psum", [128, 512], "float32"), "yn": ("psum", [128, 512], "float32"),
+    "yd": ("psum", [128, 512], "float32"), "ye": ("psum", [128, 512], "float32"),
+}
+for _k in range(len(SLICES)):
+    SCRATCH["h%d" % _k] = ("sbuf", [128, 512], "bfloat16")
+    SCRATCH["hq%d" % _k] = ("sbuf", [128, 128], "float8_e4m3fn_x4")
+    SCRATCH["hp%d" % _k] = ("sbuf", [128, 128], "uint8")
+
+SEMAPHORES = ["lx", "lw1", "lw2", "qx", "qw1", "qw2", "sent", "rx", "rm", "rn", "rln", "rld", "rle",
+              "fo", "fn", "fd", "fe", "cn", "cd", "ce", "t1", "t2", "t3", "st"]
+for _k in range(len(SLICES)):
+    SEMAPHORES += ["u%d" % _k, "v%d" % _k, "a%d" % _k, "b%d" % _k, "q%d" % _k]
+
+
+def bits(mask):
+    return [1 << i for i in range(16) if mask >> i & 1]
+
+
+def roles(core, T, topo):
+    def place(c):
+        return [k for k in T.cores if topo.host(k) == topo.host(c)].index(c)
+    out = {}
+    for c in T.cores:
+        if c == core:
+            continue
+        same = place(c) == place(core)
+        if topo.host(c) == topo.host(core):
+            out["m"] = c
+        elif topo.rack(topo.host(c)) == topo.rack(topo.host(core)):
+            if same:
+                out["n"] = c
+        elif topo.may_write(core, c):
+            out["d" if same else "e"] = c
+    return out
+
+
+def rank_program(g, core, T, topo):
+    if T.rank_of(core) is None:
+        return
+    S = T.sem
+    to = roles(core, T, topo)
+    v, a, p = g.vector, g.scalar, g.tensor
+
+    def dst(role):
+        rid, pid = topo.addr(to[role], core)
+        return DstId(rid=rid, pnc=pid)
+
+    def codes(buf, lo, n):
+        return T[buf + "q"][:, lo:lo + n].bitcast(dt.uint8)
+
+    def plane(buf, lo, n):
+        return T[buf + "p"][:, lo:lo + n]
+
+    far = topo.mask(core, to["n"]) & topo.mask(core, to["d"]) & topo.mask(core, to["e"])
+    near = topo.mask(core, to["m"]) & ~far
+    nfar, nnear = len(bits(far)), len(bits(near))
+
+    g.sync.dma_start(T.xt[:], T.x[:]).then_inc(S.lx, 16)
+    a.dma_start(T.w2t[:], T.w2[:]).then_inc(S.lw2, 16)
+    g.sync.dma_start(T.w1t[:], T.w1[:]).then_inc(S.lw1, 16)
+    v.wait_ge(S.lx, 16)
+    v.quantize_mx(T["oq"][:, 0:128], T["op"][:, 0:128], T.xt[:]).then_inc(S.qx, 1)
+    v.wait_ge(S.lw2, 16)
+    v.quantize_mx(T["oq"][:, 384:512], T["op"][:, 384:512], T.w2t[:]).then_inc(S.qw2, 1)
+    v.wait_ge(S.lw1, 16)
+    v.quantize_mx(T["oq"][:, 128:384], T["op"][:, 128:384], T.w1t[:]).then_inc(S.qw1, 1)
+
+    sent = 0
+    g.wait_ge(S.qx, 1)
+    for view in (codes, plane):
+        g.remote_dma_fused([RemoteDMATransfer(
+            srcs=[view("o", 0, 128)], dsts=[view("x", 128 * i, 128) for i in (1, 2, 0)], dst_ids=[dst(r) for r in ("d", "e", "n")],
+            dma_engine_mask=far, remote_sem=S.rx)], local_sem=S.sent)
+        sent += nfar
+    g.wait_ge(S.qw2, 1)
+    g.wait_ge(S.qw1, 1)
+    for view in (codes, plane):
+        g.remote_dma_fused([
+            RemoteDMATransfer(srcs=[view("o", 128, 384)], dsts=[view("n", 0, 384)], dst_ids=[dst("n")], dma_engine_mask=far, remote_sem=S.rn),
+            RemoteDMATransfer(srcs=[view("o", 128, 384)], dsts=[view("m", 0, 384)], dst_ids=[dst("m")], dma_engine_mask=near, remote_sem=S.rm),
+        ], local_sem=S.sent)
+        sent += nfar + nnear
+
+    W = {"o": ("o", 128), "m": ("m", 0), "n": ("n", 0)}
+    X = {"o": ("o", 0), "n": ("x", 0), "d": ("x", 128), "e": ("x", 256)}
+    Y = {"o": T.yo, "n": T.yn, "d": T.yd, "e": T.ye}
+    F = {"o": S.fo, "n": S.fn, "d": S.fd, "e": S.fe}
+    first = {c: min(k for k, s in enumerate(SLICES) if s[1] == c) for c in "onde"}
+    last = {c: max(k for k, s in enumerate(SLICES) if s[1] == c) for c in "onde"}
+    Z = [(T.za0, T.za1), (T.zb0, T.zb1)]
+    need = {"o": (S.qw1, 1), "m": (S.rm, 2 * nnear), "n": (S.rn, 2 * nfar)}
+    seen = []
+
+    def packed(buf, lo):
+        return T[buf + "q"][:, lo:lo + 128], T[buf + "p"][:, lo:lo + 128]
+
+    def once(key, sem, val):
+        if key not in seen:
+            seen.append(key)
+            p.wait_ge(sem, val)
+
+    def first_product(k):
+        r, c = SLICES[k]
+        if c == "o":
+            once("qx", S.qx, 1)
+        else:
+            once("rx", S.rx, 2 * 3 * nfar)
+        once("w" + r, *need[r])
+        if k >= 2:
+            p.wait_ge(T.sem["a%d" % (k - 2)], 2)
+            p.wait_ge(T.sem["b%d" % (k - 2)], 2)
+        (wb, wa), (xb, xa) = W[r], X[c]
+        for i, sem in enumerate(("u%d" % k, "v%d" % k)):
+            p.matmul_mx(Z[k % 2][i][:, 0:NC], *packed(wb, wa + 128 * i), *packed(xb, xa), True, True).then_inc(T.sem[sem], 1)
+
+    def second_product(k):
+        r, c = SLICES[k]
+        if r == "o":
+            once("qw2", S.qw2, 1)
+        p.wait_ge(T.sem["q%d" % k], 1)
+        wb, wa = W[r]
+        mm = p.matmul_mx(Y[c][:, 0:NC], *packed(wb, wa + 256), T["hq%d" % k][:, 0:NC], T["hp%d" % k][:, 0:NC],
+                         k == first[c], k == last[c])
+        if k == last[c]:
+            mm.then_inc(F[c], 1)
+
+    K = len(SLICES)
+    first_product(0)
+    for k in range(K):
+        if k + 1 < K:
+            first_product(k + 1)
+        second_product(k)
+
+    relu, copy = ActivationFunctionType.Relu, ActivationFunctionType.Copy
+    for k in range(K):
+        h, z = T["h%d" % k], Z[k % 2]
+        sa, sb = T.sem["a%d" % k], T.sem["b%d" % k]
+        a.wait_ge(T.sem["u%d" % k], 1)
+        a.activation(h[:, 0:512:4], z[0][:, 0:NC], relu, scale=C).then_inc(sa, 1)
+        a.activation(h[:, 1:512:4], z[0][:, 0:NC], relu, scale=-C).then_inc(sa, 1)
+        v.wait_ge(T.sem["v%d" % k], 1)
+        v.tensor_scalar(h[:, 2:512:4], z[1][:, 0:NC], C, 0.0, AluOpType.mult, AluOpType.max).then_inc(sb, 1)
+        v.tensor_scalar(h[:, 3:512:4], z[1][:, 0:NC], -C, 0.0, AluOpType.mult, AluOpType.max).then_inc(sb, 1)
+        v.wait_ge(sb, 2)
+        v.wait_ge(sa, 2)
+        v.quantize_mx(T["hq%d" % k][:, 0:NC], T["hp%d" % k][:, 0:NC], h[:]).then_inc(T.sem["q%d" % k], 1)
+        if k == last["n"] + 1:
+            a.wait_ge(S.fn, 1)
+            a.activation(T.sn[:], T.yn[:, 0:NC], copy).then_inc(S.cn, 1)
+    a.wait_ge(S.fe, 1)
+    a.activation(T.se[:], T.ye[:, 0:NC], copy).then_inc(S.ce, 1)
+    v.wait_ge(S.fd, 1)
+    v.tensor_copy(T.sd[:], T.yd[:, 0:NC]).then_inc(S.cd, 1)
+
+    g.wait_ge(S.cn, 1)
+    rid, pid = topo.addr(to["n"], core)
+    g.remote_dma(T.ln[:], T.sn[:], S.rln, S.sent, pid, rid, far)
+    sent += nfar
+    eng = bits(far)
+    half = [sum(eng[:nfar // 2]), sum(eng[nfar // 2:])]
+    g.wait_ge(S.ce, 1)
+    g.wait_ge(S.cd, 1)
+    g.remote_dma_fused([
+        RemoteDMATransfer(srcs=[T.sd[:]], dsts=[T.ld[:]], dst_ids=[dst("d")], dma_engine_mask=half[0], remote_sem=S.rld),
+        RemoteDMATransfer(srcs=[T.se[:]], dsts=[T.le[:]], dst_ids=[dst("e")], dma_engine_mask=half[1], remote_sem=S.rle),
+    ], local_sem=S.sent)
+    sent += nfar
+
+    add = AluOpType.add
+    v.wait_ge(S.fo, 1)
+    v.wait_ge(S.rln, nfar)
+    v.tensor_tensor(T.acc1[:], T.yo[:, 0:NC], T.ln[:], add).then_inc(S.t1, 1)
+    v.wait_ge(S.t1, 1)
+    v.wait_ge(S.rle, nfar // 2)
+    v.tensor_tensor(T.acc2[:], T.acc1[:], T.le[:], add).then_inc(S.t2, 1)
+    v.wait_ge(S.t2, 1)
+    v.wait_ge(S.rld, nfar // 2)
+    v.tensor_tensor(T.acc3[:], T.acc2[:], T.ld[:], add).then_inc(S.t3, 1)
+    g.sync.wait_ge(S.t3, 1)
+    g.sync.dma_start(T.y[:], T.acc3[:]).then_inc(S.st, 16)
+    g.sync.wait_ge(S.st, 16)
+    g.wait_ge(S.sent, sent)

@@ -3,17 +3,19 @@ from concourse.bass import DstId, RemoteDMATransfer
 from concourse.mybir import dt, AluOpType, ActivationFunctionType
 
 NC = 128
-SLICES = [("o", "o"), ("o", "n"), ("o", "d"), ("m", "n"), ("m", "d"), ("m", "o"), ("n", "e"), ("n", "d")]
+SLICES = [("o", "o"), ("o", "d"), ("o", "n"), ("m", "n"), ("m", "d"), ("n", "d"), ("m", "o"), ("n", "e")]
 C = float(np.float32(0.029))
+SWAPPED = ()
 
 SCRATCH = {
     "xt": ("sbuf", [128, 512], "bfloat16"),
     "w1t": ("sbuf", [128, 1024], "bfloat16"),
     "w2t": ("sbuf", [128, 512], "bfloat16"),
     "oq": ("sbuf", [128, 512], "float8_e4m3fn_x4"), "op": ("sbuf", [128, 512], "uint8"),
+    "nq": ("sbuf", [128, 512], "float8_e4m3fn_x4"), "np": ("sbuf", [128, 512], "uint8"),
     "mq": ("sbuf", [128, 384], "float8_e4m3fn_x4"), "mp": ("sbuf", [128, 384], "uint8"),
-    "nq": ("sbuf", [128, 384], "float8_e4m3fn_x4"), "np": ("sbuf", [128, 384], "uint8"),
-    "xq": ("sbuf", [128, 384], "float8_e4m3fn_x4"), "xp": ("sbuf", [128, 384], "uint8"),
+    "dq": ("sbuf", [128, 128], "float8_e4m3fn_x4"), "dp": ("sbuf", [128, 128], "uint8"),
+    "eq": ("sbuf", [128, 128], "float8_e4m3fn_x4"), "ep": ("sbuf", [128, 128], "uint8"),
     "sn": ("sbuf", [128, 128], "float32"), "sd": ("sbuf", [128, 128], "float32"), "se": ("sbuf", [128, 128], "float32"),
     "ln": ("sbuf", [128, 128], "float32"), "ld": ("sbuf", [128, 128], "float32"), "le": ("sbuf", [128, 128], "float32"),
     "acc1": ("sbuf", [128, 128], "float32"), "acc2": ("sbuf", [128, 128], "float32"), "acc3": ("sbuf", [128, 128], "float32"),
@@ -27,7 +29,7 @@ for _k in range(len(SLICES)):
     SCRATCH["hq%d" % _k] = ("sbuf", [128, 128], "float8_e4m3fn_x4")
     SCRATCH["hp%d" % _k] = ("sbuf", [128, 128], "uint8")
 
-SEMAPHORES = ["lx", "lw1", "lw2", "qx", "qw1", "qw2", "sent", "rx", "rm", "rn", "rln", "rld", "rle",
+SEMAPHORES = ["lx", "lw1", "lw2", "qx", "qw1", "qw2", "sent", "rxc", "rxp", "rnp", "rnw", "rm", "rxe", "rln", "rld", "rle",
               "fo", "fn", "fd", "fe", "cn", "cd", "ce", "t1", "t2", "t3", "st"]
 for _k in range(len(SLICES)):
     SEMAPHORES += ["u%d" % _k, "v%d" % _k, "a%d" % _k, "b%d" % _k, "q%d" % _k]
@@ -37,21 +39,25 @@ def bits(mask):
     return [1 << i for i in range(16) if mask >> i & 1]
 
 
+def place(c, T, topo):
+    return [k for k in T.cores if topo.host(k) == topo.host(c)].index(c)
+
+
 def roles(core, T, topo):
-    def place(c):
-        return [k for k in T.cores if topo.host(k) == topo.host(c)].index(c)
+    mine = place(core, T, topo)
     out = {}
     for c in T.cores:
         if c == core:
             continue
-        same = place(c) == place(core)
+        same = place(c, T, topo) == mine
         if topo.host(c) == topo.host(core):
             out["m"] = c
-        elif topo.rack(topo.host(c)) == topo.rack(topo.host(core)):
-            if same:
-                out["n"] = c
         elif topo.may_write(core, c):
-            out["d" if same else "e"] = c
+            rack = topo.rack(topo.host(c)) == topo.rack(topo.host(core))
+            if rack == (mine in SWAPPED):
+                out["d" if same else "e"] = c
+            elif same:
+                out["n"] = c
     return out
 
 
@@ -72,7 +78,7 @@ def rank_program(g, core, T, topo):
     def plane(buf, lo, n):
         return T[buf + "p"][:, lo:lo + n]
 
-    far = topo.mask(core, to["n"]) & topo.mask(core, to["d"]) & topo.mask(core, to["e"])
+    far = topo.mask(core, to["n"]) & topo.mask(core, to["d"])
     near = topo.mask(core, to["m"]) & ~far
     nfar, nnear = len(bits(far)), len(bits(near))
 
@@ -86,58 +92,63 @@ def rank_program(g, core, T, topo):
     v.wait_ge(S.lw1, 16)
     v.quantize_mx(T["oq"][:, 128:384], T["op"][:, 128:384], T.w1t[:]).then_inc(S.qw1, 1)
 
-    sent = 0
+    sent = [0]
+
+    def send(*parts):
+        g.remote_dma_fused([RemoteDMATransfer(srcs=[s], dsts=[t] * len(rs) if not isinstance(t, list) else t, dst_ids=[dst(r) for r in rs],
+                                              dma_engine_mask=m, remote_sem=sem) for s, t, rs, m, sem in parts], local_sem=S.sent)
+        sent[0] += sum(len(bits(q[3])) for q in parts)
+
     g.wait_ge(S.qx, 1)
-    for view in (codes, plane):
-        g.remote_dma_fused([RemoteDMATransfer(
-            srcs=[view("o", 0, 128)], dsts=[view("x", 128 * i, 128) for i in (1, 2, 0)], dst_ids=[dst(r) for r in ("d", "e", "n")],
-            dma_engine_mask=far, remote_sem=S.rx)], local_sem=S.sent)
-        sent += nfar
+    send((codes("o", 0, 128), [codes("d", 0, 128), codes("n", 0, 128)], "dn", far, S.rxc))
+    send((plane("o", 0, 128), plane("d", 0, 128), "d", far, S.rxp))
     g.wait_ge(S.qw2, 1)
     g.wait_ge(S.qw1, 1)
+    send((plane("o", 0, 512), plane("n", 0, 512), "n", far, S.rnp))
+    send((codes("o", 128, 384), codes("n", 128, 384), "n", far, S.rnw), (codes("o", 128, 384), codes("m", 0, 384), "m", near, S.rm))
+    send((plane("o", 128, 384), plane("m", 0, 384), "m", near, S.rm))
+    have = {"xo": [(S.qx, 1)], "xd": [(S.rxc, 2 * nfar), (S.rxp, nfar)], "xn": [(S.rxc, 2 * nfar), (S.rnp, nfar)],
+            "xe": [(S.rxe, 2 * nnear)],
+            "wo": [(S.qw1, 1)], "wm": [(S.rm, 2 * nnear)], "wn": [(S.rnp, nfar), (S.rnw, nfar)]}
+    on = "n" if len(SWAPPED) == 1 else "d"
+    for sem, val in have["x" + on]:
+        g.wait_ge(sem, val)
     for view in (codes, plane):
-        g.remote_dma_fused([
-            RemoteDMATransfer(srcs=[view("o", 128, 384)], dsts=[view("n", 0, 384)], dst_ids=[dst("n")], dma_engine_mask=far, remote_sem=S.rn),
-            RemoteDMATransfer(srcs=[view("o", 128, 384)], dsts=[view("m", 0, 384)], dst_ids=[dst("m")], dma_engine_mask=near, remote_sem=S.rm),
-        ], local_sem=S.sent)
-        sent += nfar + nnear
+        send((view(on, 0, 128), view("e", 0, 128), "m", near, S.rxe))
 
-    W = {"o": ("o", 128), "m": ("m", 0), "n": ("n", 0)}
-    X = {"o": ("o", 0), "n": ("x", 0), "d": ("x", 128), "e": ("x", 256)}
+    W = {"o": ("o", 128), "m": ("m", 0), "n": ("n", 128)}
     Y = {"o": T.yo, "n": T.yn, "d": T.yd, "e": T.ye}
     F = {"o": S.fo, "n": S.fn, "d": S.fd, "e": S.fe}
     first = {c: min(k for k, s in enumerate(SLICES) if s[1] == c) for c in "onde"}
     last = {c: max(k for k, s in enumerate(SLICES) if s[1] == c) for c in "onde"}
+    outs = sorted((c for c in "nde"), key=lambda c: last[c])
     Z = [(T.za0, T.za1), (T.zb0, T.zb1)]
-    need = {"o": (S.qw1, 1), "m": (S.rm, 2 * nnear), "n": (S.rn, 2 * nfar)}
+    K = len(SLICES)
     seen = []
 
     def packed(buf, lo):
         return T[buf + "q"][:, lo:lo + 128], T[buf + "p"][:, lo:lo + 128]
 
-    def once(key, sem, val):
-        if key not in seen:
-            seen.append(key)
-            p.wait_ge(sem, val)
+    def once(waits):
+        for w in waits:
+            if w not in seen:
+                seen.append(w)
+                p.wait_ge(*w)
 
     def first_product(k):
         r, c = SLICES[k]
-        if c == "o":
-            once("qx", S.qx, 1)
-        else:
-            once("rx", S.rx, 2 * 3 * nfar)
-        once("w" + r, *need[r])
+        once(have["x" + c] + have["w" + r])
         if k >= 2:
             p.wait_ge(T.sem["a%d" % (k - 2)], 2)
             p.wait_ge(T.sem["b%d" % (k - 2)], 2)
-        (wb, wa), (xb, xa) = W[r], X[c]
+        wb, wa = W[r]
         for i, sem in enumerate(("u%d" % k, "v%d" % k)):
-            p.matmul_mx(Z[k % 2][i][:, 0:NC], *packed(wb, wa + 128 * i), *packed(xb, xa), True, True).then_inc(T.sem[sem], 1)
+            p.matmul_mx(Z[k % 2][i][:, 0:NC], *packed(wb, wa + 128 * i), *packed(c, 0), True, True).then_inc(T.sem[sem], 1)
 
     def second_product(k):
         r, c = SLICES[k]
         if r == "o":
-            once("qw2", S.qw2, 1)
+            once([(S.qw2, 1)])
         p.wait_ge(T.sem["q%d" % k], 1)
         wb, wa = W[r]
         mm = p.matmul_mx(Y[c][:, 0:NC], *packed(wb, wa + 256), T["hq%d" % k][:, 0:NC], T["hp%d" % k][:, 0:NC],
@@ -145,7 +156,6 @@ def rank_program(g, core, T, topo):
         if k == last[c]:
             mm.then_inc(F[c], 1)
 
-    K = len(SLICES)
     first_product(0)
     for k in range(K):
         if k + 1 < K:
@@ -153,6 +163,12 @@ def rank_program(g, core, T, topo):
         second_product(k)
 
     relu, copy = ActivationFunctionType.Relu, ActivationFunctionType.Copy
+    STAGE = {"n": (T.sn, T.ln, S.cn, S.rln), "d": (T.sd, T.ld, S.cd, S.rld), "e": (T.se, T.le, S.ce, S.rle)}
+
+    def to_sbuf(c):
+        a.wait_ge(F[c], 1)
+        a.activation(STAGE[c][0][:], Y[c][:, 0:NC], copy).then_inc(STAGE[c][2], 1)
+
     for k in range(K):
         h, z = T["h%d" % k], Z[k % 2]
         sa, sb = T.sem["a%d" % k], T.sem["b%d" % k]
@@ -165,39 +181,28 @@ def rank_program(g, core, T, topo):
         v.wait_ge(sb, 2)
         v.wait_ge(sa, 2)
         v.quantize_mx(T["hq%d" % k][:, 0:NC], T["hp%d" % k][:, 0:NC], h[:]).then_inc(T.sem["q%d" % k], 1)
-        if k == last["n"] + 1:
-            a.wait_ge(S.fn, 1)
-            a.activation(T.sn[:], T.yn[:, 0:NC], copy).then_inc(S.cn, 1)
-    a.wait_ge(S.fe, 1)
-    a.activation(T.se[:], T.ye[:, 0:NC], copy).then_inc(S.ce, 1)
-    v.wait_ge(S.fd, 1)
-    v.tensor_copy(T.sd[:], T.yd[:, 0:NC]).then_inc(S.cd, 1)
+        for c in outs:
+            if last[c] == k - 1:
+                to_sbuf(c)
+    for c in outs:
+        if last[c] == K - 1:
+            to_sbuf(c)
 
-    g.wait_ge(S.cn, 1)
-    rid, pid = topo.addr(to["n"], core)
-    g.remote_dma(T.ln[:], T.sn[:], S.rln, S.sent, pid, rid, far)
-    sent += nfar
-    eng = bits(far)
-    half = [sum(eng[:nfar // 2]), sum(eng[nfar // 2:])]
-    g.wait_ge(S.ce, 1)
-    g.wait_ge(S.cd, 1)
-    g.remote_dma_fused([
-        RemoteDMATransfer(srcs=[T.sd[:]], dsts=[T.ld[:]], dst_ids=[dst("d")], dma_engine_mask=half[0], remote_sem=S.rld),
-        RemoteDMATransfer(srcs=[T.se[:]], dsts=[T.le[:]], dst_ids=[dst("e")], dma_engine_mask=half[1], remote_sem=S.rle),
-    ], local_sem=S.sent)
-    sent += nfar
+    for c in outs:
+        s, t, ready, rsem = STAGE[c]
+        g.wait_ge(ready, 1)
+        send((s[:], t[:], c, far, rsem))
 
-    add = AluOpType.add
     v.wait_ge(S.fo, 1)
-    v.wait_ge(S.rln, nfar)
-    v.tensor_tensor(T.acc1[:], T.yo[:, 0:NC], T.ln[:], add).then_inc(S.t1, 1)
-    v.wait_ge(S.t1, 1)
-    v.wait_ge(S.rle, nfar // 2)
-    v.tensor_tensor(T.acc2[:], T.acc1[:], T.le[:], add).then_inc(S.t2, 1)
-    v.wait_ge(S.t2, 1)
-    v.wait_ge(S.rld, nfar // 2)
-    v.tensor_tensor(T.acc3[:], T.acc2[:], T.ld[:], add).then_inc(S.t3, 1)
+    acc = T.yo[:, 0:NC]
+    for i, c in enumerate(outs):
+        if i:
+            v.wait_ge(T.sem["t%d" % i], 1)
+        v.wait_ge(STAGE[c][3], nfar)
+        out = T["acc%d" % (i + 1)][:]
+        v.tensor_tensor(out, acc, STAGE[c][1][:], AluOpType.add).then_inc(T.sem["t%d" % (i + 1)], 1)
+        acc = out
     g.sync.wait_ge(S.t3, 1)
     g.sync.dma_start(T.y[:], T.acc3[:]).then_inc(S.st, 16)
     g.sync.wait_ge(S.st, 16)
-    g.wait_ge(S.sent, sent)
+    g.wait_ge(S.sent, sent[0])

@@ -3,25 +3,23 @@ from concourse.bass import DstId, RemoteDMATransfer
 from concourse.mybir import dt, AluOpType, ActivationFunctionType
 
 NC = 128
-SLICES = [("o", "o"), ("o", "d"), ("o", "n"), ("m", "n"), ("m", "d"), ("n", "d"), ("m", "o"), ("n", "e")]
+SLICES = [("o", "o"), ("o", "d"), ("o", "m"), ("n", "d"), ("n", "m"), ("o", "e"), ("n", "e"), ("n", "o")]
 C = float(np.float32(0.029))
-SWAPPED = ()
 
 SCRATCH = {
     "xt": ("sbuf", [128, 512], "bfloat16"),
     "w1t": ("sbuf", [128, 1024], "bfloat16"),
     "w2t": ("sbuf", [128, 512], "bfloat16"),
-    "oq": ("sbuf", [128, 512], "float8_e4m3fn_x4"), "op": ("sbuf", [128, 512], "uint8"),
-    "nq": ("sbuf", [128, 512], "float8_e4m3fn_x4"), "np": ("sbuf", [128, 512], "uint8"),
-    "mq": ("sbuf", [128, 384], "float8_e4m3fn_x4"), "mp": ("sbuf", [128, 384], "uint8"),
-    "dq": ("sbuf", [128, 128], "float8_e4m3fn_x4"), "dp": ("sbuf", [128, 128], "uint8"),
-    "eq": ("sbuf", [128, 128], "float8_e4m3fn_x4"), "ep": ("sbuf", [128, 128], "uint8"),
-    "sn": ("sbuf", [128, 128], "float32"), "sd": ("sbuf", [128, 128], "float32"), "se": ("sbuf", [128, 128], "float32"),
-    "ln": ("sbuf", [128, 128], "float32"), "ld": ("sbuf", [128, 128], "float32"), "le": ("sbuf", [128, 128], "float32"),
+    "xq": ("sbuf", [128, 256], "float8_e4m3fn_x4"), "xp": ("sbuf", [128, 256], "uint8"),
+    "zq": ("sbuf", [128, 256], "float8_e4m3fn_x4"), "zp": ("sbuf", [128, 256], "uint8"),
+    "oq": ("sbuf", [128, 384], "float8_e4m3fn_x4"), "op": ("sbuf", [128, 384], "uint8"),
+    "nq": ("sbuf", [128, 384], "float8_e4m3fn_x4"), "np": ("sbuf", [128, 384], "uint8"),
+    "sm": ("sbuf", [128, 128], "float32"), "sd": ("sbuf", [128, 128], "float32"), "se": ("sbuf", [128, 128], "float32"),
+    "lm": ("sbuf", [128, 128], "float32"), "ld": ("sbuf", [128, 128], "float32"), "le": ("sbuf", [128, 128], "float32"),
     "acc1": ("sbuf", [128, 128], "float32"), "acc2": ("sbuf", [128, 128], "float32"), "acc3": ("sbuf", [128, 128], "float32"),
     "za0": ("psum", [128, 512], "float32"), "za1": ("psum", [128, 512], "float32"),
     "zb0": ("psum", [128, 512], "float32"), "zb1": ("psum", [128, 512], "float32"),
-    "yo": ("psum", [128, 512], "float32"), "yn": ("psum", [128, 512], "float32"),
+    "yo": ("psum", [128, 512], "float32"), "ym": ("psum", [128, 512], "float32"),
     "yd": ("psum", [128, 512], "float32"), "ye": ("psum", [128, 512], "float32"),
 }
 for _k in range(len(SLICES)):
@@ -29,8 +27,8 @@ for _k in range(len(SLICES)):
     SCRATCH["hq%d" % _k] = ("sbuf", [128, 128], "float8_e4m3fn_x4")
     SCRATCH["hp%d" % _k] = ("sbuf", [128, 128], "uint8")
 
-SEMAPHORES = ["lx", "lw1", "lw2", "qx", "qw1", "qw2", "sent", "rxc", "rxp", "rnp", "rnw", "rm", "rxe", "rln", "rld", "rle",
-              "fo", "fn", "fd", "fe", "cn", "cd", "ce", "t1", "t2", "t3", "st"]
+SEMAPHORES = ["lx", "lw1", "lw2", "qx", "qw1", "qw2", "sent", "rxd", "rxm", "rxe", "rn", "rlm", "rld", "rle",
+              "fo", "fm", "fd", "fe", "cm", "cd", "ce", "t1", "t2", "t3", "st"]
 for _k in range(len(SLICES)):
     SEMAPHORES += ["u%d" % _k, "v%d" % _k, "a%d" % _k, "b%d" % _k, "q%d" % _k]
 
@@ -44,20 +42,18 @@ def place(c, T, topo):
 
 
 def roles(core, T, topo):
-    mine = place(core, T, topo)
     out = {}
     for c in T.cores:
         if c == core:
             continue
-        same = place(c, T, topo) == mine
+        same = place(c, T, topo) == place(core, T, topo)
         if topo.host(c) == topo.host(core):
             out["m"] = c
-        elif topo.may_write(core, c):
-            rack = topo.rack(topo.host(c)) == topo.rack(topo.host(core))
-            if rack == (mine in SWAPPED):
-                out["d" if same else "e"] = c
-            elif same:
+        elif topo.rack(topo.host(c)) == topo.rack(topo.host(core)):
+            if same:
                 out["n"] = c
+        elif topo.may_write(core, c):
+            out["d" if same else "e"] = c
     return out
 
 
@@ -78,50 +74,47 @@ def rank_program(g, core, T, topo):
     def plane(buf, lo, n):
         return T[buf + "p"][:, lo:lo + n]
 
-    far = topo.mask(core, to["n"]) & topo.mask(core, to["d"])
+    far = topo.mask(core, to["n"]) & topo.mask(core, to["d"]) & topo.mask(core, to["e"])
     near = topo.mask(core, to["m"]) & ~far
     nfar, nnear = len(bits(far)), len(bits(near))
 
     g.sync.dma_start(T.xt[:], T.x[:]).then_inc(S.lx, 16)
-    a.dma_start(T.w2t[:], T.w2[:]).then_inc(S.lw2, 16)
     g.sync.dma_start(T.w1t[:], T.w1[:]).then_inc(S.lw1, 16)
+    g.sync.dma_start(T.w2t[:], T.w2[:]).then_inc(S.lw2, 16)
     v.wait_ge(S.lx, 16)
-    v.quantize_mx(T["oq"][:, 0:128], T["op"][:, 0:128], T.xt[:]).then_inc(S.qx, 1)
-    v.wait_ge(S.lw2, 16)
-    v.quantize_mx(T["oq"][:, 384:512], T["op"][:, 384:512], T.w2t[:]).then_inc(S.qw2, 1)
+    v.quantize_mx(T["xq"][:, 0:128], T["xp"][:, 0:128], T.xt[:]).then_inc(S.qx, 1)
     v.wait_ge(S.lw1, 16)
-    v.quantize_mx(T["oq"][:, 128:384], T["op"][:, 128:384], T.w1t[:]).then_inc(S.qw1, 1)
+    v.quantize_mx(T["oq"][:, 0:256], T["op"][:, 0:256], T.w1t[:]).then_inc(S.qw1, 1)
+    v.wait_ge(S.lw2, 16)
+    v.quantize_mx(T["oq"][:, 256:384], T["op"][:, 256:384], T.w2t[:]).then_inc(S.qw2, 1)
 
     sent = [0]
 
     def send(*parts):
-        g.remote_dma_fused([RemoteDMATransfer(srcs=[s], dsts=[t] * len(rs) if not isinstance(t, list) else t, dst_ids=[dst(r) for r in rs],
-                                              dma_engine_mask=m, remote_sem=sem) for s, t, rs, m, sem in parts], local_sem=S.sent)
+        g.remote_dma_fused([RemoteDMATransfer(srcs=[s], dsts=[t], dst_ids=[dst(r)], dma_engine_mask=m, remote_sem=sem)
+                            for s, t, r, m, sem in parts], local_sem=S.sent)
         sent[0] += sum(len(bits(q[3])) for q in parts)
 
     g.wait_ge(S.qx, 1)
-    send((codes("o", 0, 128), [codes("d", 0, 128), codes("n", 0, 128)], "dn", far, S.rxc))
-    send((plane("o", 0, 128), plane("d", 0, 128), "d", far, S.rxp))
-    g.wait_ge(S.qw2, 1)
+    send((codes("x", 0, 128), codes("x", 128, 128), "d", far, S.rxd))
+    send((plane("x", 0, 128), plane("x", 128, 128), "d", far, S.rxd), (plane("x", 0, 128), plane("z", 0, 128), "m", near, S.rxm))
     g.wait_ge(S.qw1, 1)
-    send((plane("o", 0, 512), plane("n", 0, 512), "n", far, S.rnp))
-    send((codes("o", 128, 384), codes("n", 128, 384), "n", far, S.rnw), (codes("o", 128, 384), codes("m", 0, 384), "m", near, S.rm))
-    send((plane("o", 128, 384), plane("m", 0, 384), "m", near, S.rm))
-    have = {"xo": [(S.qx, 1)], "xd": [(S.rxc, 2 * nfar), (S.rxp, nfar)], "xn": [(S.rxc, 2 * nfar), (S.rnp, nfar)],
-            "xe": [(S.rxe, 2 * nnear)],
-            "wo": [(S.qw1, 1)], "wm": [(S.rm, 2 * nnear)], "wn": [(S.rnp, nfar), (S.rnw, nfar)]}
-    on = "n" if len(SWAPPED) == 1 else "d"
-    for sem, val in have["x" + on]:
-        g.wait_ge(sem, val)
-    for view in (codes, plane):
-        send((view(on, 0, 128), view("e", 0, 128), "m", near, S.rxe))
+    g.wait_ge(S.qw2, 1)
+    send((codes("o", 0, 384), codes("n", 0, 384), "n", far, S.rn))
+    send((plane("o", 0, 384), plane("n", 0, 384), "n", far, S.rn))
+    send((codes("x", 0, 128), codes("z", 0, 128), "m", near, S.rxm))
+    g.wait_ge(S.rxd, 2 * nfar)
+    send((codes("x", 128, 128), codes("z", 128, 128), "m", near, S.rxe))
+    send((plane("x", 128, 128), plane("z", 128, 128), "m", near, S.rxe))
 
-    W = {"o": ("o", 128), "m": ("m", 0), "n": ("n", 128)}
-    Y = {"o": T.yo, "n": T.yn, "d": T.yd, "e": T.ye}
-    F = {"o": S.fo, "n": S.fn, "d": S.fd, "e": S.fe}
-    first = {c: min(k for k, s in enumerate(SLICES) if s[1] == c) for c in "onde"}
-    last = {c: max(k for k, s in enumerate(SLICES) if s[1] == c) for c in "onde"}
-    outs = sorted((c for c in "nde"), key=lambda c: last[c])
+    X = {"o": ("x", 0), "d": ("x", 128), "m": ("z", 0), "e": ("z", 128)}
+    x_here = {"o": (S.qx, 1), "d": (S.rxd, 2 * nfar), "m": (S.rxm, 2 * nnear), "e": (S.rxe, 2 * nnear)}
+    w_here = {"o": [(S.qw1, 1)], "n": [(S.rn, 2 * nfar)]}
+    Y = {"o": T.yo, "m": T.ym, "d": T.yd, "e": T.ye}
+    F = {"o": S.fo, "m": S.fm, "d": S.fd, "e": S.fe}
+    first = {c: min(k for k, s in enumerate(SLICES) if s[1] == c) for c in "omde"}
+    last = {c: max(k for k, s in enumerate(SLICES) if s[1] == c) for c in "omde"}
+    outs = sorted("mde", key=lambda c: last[c])
     Z = [(T.za0, T.za1), (T.zb0, T.zb1)]
     K = len(SLICES)
     seen = []
@@ -137,21 +130,19 @@ def rank_program(g, core, T, topo):
 
     def first_product(k):
         r, c = SLICES[k]
-        once(have["x" + c] + have["w" + r])
+        once([x_here[c]] + w_here[r])
         if k >= 2:
             p.wait_ge(T.sem["a%d" % (k - 2)], 2)
             p.wait_ge(T.sem["b%d" % (k - 2)], 2)
-        wb, wa = W[r]
         for i, sem in enumerate(("u%d" % k, "v%d" % k)):
-            p.matmul_mx(Z[k % 2][i][:, 0:NC], *packed(wb, wa + 128 * i), *packed(c, 0), True, True).then_inc(T.sem[sem], 1)
+            p.matmul_mx(Z[k % 2][i][:, 0:NC], *packed(r, 128 * i), *packed(*X[c]), True, True).then_inc(T.sem[sem], 1)
 
     def second_product(k):
         r, c = SLICES[k]
         if r == "o":
             once([(S.qw2, 1)])
         p.wait_ge(T.sem["q%d" % k], 1)
-        wb, wa = W[r]
-        mm = p.matmul_mx(Y[c][:, 0:NC], *packed(wb, wa + 256), T["hq%d" % k][:, 0:NC], T["hp%d" % k][:, 0:NC],
+        mm = p.matmul_mx(Y[c][:, 0:NC], *packed(r, 256), T["hq%d" % k][:, 0:NC], T["hp%d" % k][:, 0:NC],
                          k == first[c], k == last[c])
         if k == last[c]:
             mm.then_inc(F[c], 1)
@@ -163,11 +154,7 @@ def rank_program(g, core, T, topo):
         second_product(k)
 
     relu, copy = ActivationFunctionType.Relu, ActivationFunctionType.Copy
-    STAGE = {"n": (T.sn, T.ln, S.cn, S.rln), "d": (T.sd, T.ld, S.cd, S.rld), "e": (T.se, T.le, S.ce, S.rle)}
-
-    def to_sbuf(c):
-        a.wait_ge(F[c], 1)
-        a.activation(STAGE[c][0][:], Y[c][:, 0:NC], copy).then_inc(STAGE[c][2], 1)
+    STAGE = {"m": (T.sm, T.lm, S.cm, S.rlm), "d": (T.sd, T.ld, S.cd, S.rld), "e": (T.se, T.le, S.ce, S.rle)}
 
     for k in range(K):
         h, z = T["h%d" % k], Z[k % 2]
@@ -183,22 +170,20 @@ def rank_program(g, core, T, topo):
         v.quantize_mx(T["hq%d" % k][:, 0:NC], T["hp%d" % k][:, 0:NC], h[:]).then_inc(T.sem["q%d" % k], 1)
         for c in outs:
             if last[c] == k - 1:
-                to_sbuf(c)
-    for c in outs:
-        if last[c] == K - 1:
-            to_sbuf(c)
+                a.wait_ge(F[c], 1)
+                a.activation(STAGE[c][0][:], Y[c][:, 0:NC], copy).then_inc(STAGE[c][2], 1)
 
     for c in outs:
         s, t, ready, rsem = STAGE[c]
         g.wait_ge(ready, 1)
-        send((s[:], t[:], c, far, rsem))
+        send((s[:], t[:], c, near if c == "m" else far, rsem))
 
     v.wait_ge(S.fo, 1)
     acc = T.yo[:, 0:NC]
     for i, c in enumerate(outs):
         if i:
             v.wait_ge(T.sem["t%d" % i], 1)
-        v.wait_ge(STAGE[c][3], nfar)
+        v.wait_ge(STAGE[c][3], nnear if c == "m" else nfar)
         out = T["acc%d" % (i + 1)][:]
         v.tensor_tensor(out, acc, STAGE[c][1][:], AluOpType.add).then_inc(T.sem["t%d" % (i + 1)], 1)
         acc = out

import numpy as np
from concourse.bass import DstId, RemoteDMATransfer
from concourse.mybir import dt, AluOpType, ActivationFunctionType

NC = 128
SLICES = [("o", "o"), ("o", "d"), ("o", "m"), ("n", "d"), ("n", "m"), ("o", "e"), ("n", "e"), ("n", "o")]
C = float(np.float32(0.029))

SCRATCH = {
    "xt": ("sbuf", [128, 512], "bfloat16"),
    "w1t": ("sbuf", [128, 1024], "bfloat16"),
    "w2t": ("sbuf", [128, 512], "bfloat16"),
    "xq": ("sbuf", [128, 256], "float8_e4m3fn_x4"), "xp": ("sbuf", [128, 256], "uint8"),
    "zq": ("sbuf", [128, 256], "float8_e4m3fn_x4"), "zp": ("sbuf", [128, 256], "uint8"),
    "oq": ("sbuf", [128, 384], "float8_e4m3fn_x4"), "op": ("sbuf", [128, 384], "uint8"),
    "nq": ("sbuf", [128, 384], "float8_e4m3fn_x4"), "np": ("sbuf", [128, 384], "uint8"),
    "sm": ("sbuf", [128, 128], "float32"), "sd": ("sbuf", [128, 128], "float32"), "se": ("sbuf", [128, 128], "float32"),
    "lm": ("sbuf", [128, 128], "float32"), "ld": ("sbuf", [128, 128], "float32"), "le": ("sbuf", [128, 128], "float32"),
    "acc1": ("sbuf", [128, 128], "float32"), "acc2": ("sbuf", [128, 128], "float32"), "acc3": ("sbuf", [128, 128], "float32"),
    "za0": ("psum", [128, 512], "float32"), "za1": ("psum", [128, 512], "float32"),
    "zb0": ("psum", [128, 512], "float32"), "zb1": ("psum", [128, 512], "float32"),
    "yo": ("psum", [128, 512], "float32"), "ym": ("psum", [128, 512], "float32"),
    "yd": ("psum", [128, 512], "float32"), "ye": ("psum", [128, 512], "float32"),
}
for _k in range(len(SLICES)):
    SCRATCH["h%d" % _k] = ("sbuf", [128, 512], "bfloat16")
    SCRATCH["hq%d" % _k] = ("sbuf", [128, 128], "float8_e4m3fn_x4")
    SCRATCH["hp%d" % _k] = ("sbuf", [128, 128], "uint8")

SEMAPHORES = ["lx", "lw1", "lw2", "qx", "qw1", "qw2", "sent", "rxd", "rxm", "rxe", "rn", "rlm", "rld", "rle",
              "fo", "fm", "fd", "fe", "cm", "cd", "ce", "t1", "t2", "t3", "st"]
for _k in range(len(SLICES)):
    SEMAPHORES += ["u%d" % _k, "v%d" % _k, "a%d" % _k, "b%d" % _k, "q%d" % _k]


def bits(mask):
    return [1 << i for i in range(16) if mask >> i & 1]


def place(c, T, topo):
    return [k for k in T.cores if topo.host(k) == topo.host(c)].index(c)


def roles(core, T, topo):
    out = {}
    for c in T.cores:
        if c == core:
            continue
        same = place(c, T, topo) == place(core, T, topo)
        if topo.host(c) == topo.host(core):
            out["m"] = c
        elif topo.rack(topo.host(c)) == topo.rack(topo.host(core)):
            if same:
                out["n"] = c
        elif topo.may_write(core, c):
            out["d" if same else "e"] = c
    return out


def rank_program(g, core, T, topo):
    if T.rank_of(core) is None:
        return
    S = T.sem
    to = roles(core, T, topo)
    v, a, p = g.vector, g.scalar, g.tensor

    def dst(role):
        rid, pid = topo.addr(to[role], core)
        return DstId(rid=rid, pnc=pid)

    def codes(buf, lo, n):
        return T[buf + "q"][:, lo:lo + n].bitcast(dt.uint8)

    def plane(buf, lo, n):
        return T[buf + "p"][:, lo:lo + n]

    far = topo.mask(core, to["n"]) & topo.mask(core, to["d"]) & topo.mask(core, to["e"])
    near = topo.mask(core, to["m"]) & ~far
    nfar, nnear = len(bits(far)), len(bits(near))

    g.sync.dma_start(T.xt[:], T.x[:]).then_inc(S.lx, 16)
    g.sync.dma_start(T.w1t[:], T.w1[:]).then_inc(S.lw1, 16)
    g.sync.dma_start(T.w2t[:], T.w2[:]).then_inc(S.lw2, 16)
    v.wait_ge(S.lx, 16)
    v.quantize_mx(T["xq"][:, 0:128], T["xp"][:, 0:128], T.xt[:]).then_inc(S.qx, 1)
    v.wait_ge(S.lw1, 16)
    v.quantize_mx(T["oq"][:, 0:256], T["op"][:, 0:256], T.w1t[:]).then_inc(S.qw1, 1)
    v.wait_ge(S.lw2, 16)
    v.quantize_mx(T["oq"][:, 256:384], T["op"][:, 256:384], T.w2t[:]).then_inc(S.qw2, 1)

    sent = [0]

    def send(*parts):
        g.remote_dma_fused([RemoteDMATransfer(srcs=[s], dsts=[t], dst_ids=[dst(r)], dma_engine_mask=m, remote_sem=sem)
                            for s, t, r, m, sem in parts], local_sem=S.sent)
        sent[0] += sum(len(bits(q[3])) for q in parts)

    g.wait_ge(S.qx, 1)
    send((codes("x", 0, 128), codes("x", 128, 128), "d", far, S.rxd))
    send((plane("x", 0, 128), plane("x", 128, 128), "d", far, S.rxd), (plane("x", 0, 128), plane("z", 0, 128), "m", near, S.rxm))
    g.wait_ge(S.qw1, 1)
    g.wait_ge(S.qw2, 1)
    send((codes("o", 0, 384), codes("n", 0, 384), "n", far, S.rn))
    send((plane("o", 0, 384), plane("n", 0, 384), "n", far, S.rn))
    send((codes("x", 0, 128), codes("z", 0, 128), "m", near, S.rxm))
    g.wait_ge(S.rxd, 2 * nfar)
    send((codes("x", 128, 128), codes("z", 128, 128), "m", near, S.rxe))
    send((plane("x", 128, 128), plane("z", 128, 128), "m", near, S.rxe))

    X = {"o": ("x", 0), "d": ("x", 128), "m": ("z", 0), "e": ("z", 128)}
    x_here = {"o": (S.qx, 1), "d": (S.rxd, 2 * nfar), "m": (S.rxm, 2 * nnear), "e": (S.rxe, 2 * nnear)}
    w_here = {"o": [(S.qw1, 1)], "n": [(S.rn, 2 * nfar)]}
    Y = {"o": T.yo, "m": T.ym, "d": T.yd, "e": T.ye}
    F = {"o": S.fo, "m": S.fm, "d": S.fd, "e": S.fe}
    first = {c: min(k for k, s in enumerate(SLICES) if s[1] == c) for c in "omde"}
    last = {c: max(k for k, s in enumerate(SLICES) if s[1] == c) for c in "omde"}
    outs = sorted("mde", key=lambda c: last[c])
    Z = [(T.za0, T.za1), (T.zb0, T.zb1)]
    K = len(SLICES)
    seen = []

    def packed(buf, lo):
        return T[buf + "q"][:, lo:lo + 128], T[buf + "p"][:, lo:lo + 128]

    def once(waits):
        for w in waits:
            if w not in seen:
                seen.append(w)
                p.wait_ge(*w)

    def first_product(k):
        r, c = SLICES[k]
        once([x_here[c]] + w_here[r])
        if k >= 2:
            p.wait_ge(T.sem["a%d" % (k - 2)], 2)
            p.wait_ge(T.sem["b%d" % (k - 2)], 2)
        for i, sem in enumerate(("u%d" % k, "v%d" % k)):
            p.matmul_mx(Z[k % 2][i][:, 0:NC], *packed(r, 128 * i), *packed(*X[c]), True, True).then_inc(T.sem[sem], 1)

    def second_product(k):
        r, c = SLICES[k]
        if r == "o":
            once([(S.qw2, 1)])
        p.wait_ge(T.sem["q%d" % k], 1)
        mm = p.matmul_mx(Y[c][:, 0:NC], *packed(r, 256), T["hq%d" % k][:, 0:NC], T["hp%d" % k][:, 0:NC],
                         k == first[c], k == last[c])
        if k == last[c]:
            mm.then_inc(F[c], 1)

    first_product(0)
    for k in range(K):
        if k + 1 < K:
            first_product(k + 1)
        second_product(k)

    relu, copy = ActivationFunctionType.Relu, ActivationFunctionType.Copy
    STAGE = {"m": (T.sm, T.lm, S.cm, S.rlm), "d": (T.sd, T.ld, S.cd, S.rld), "e": (T.se, T.le, S.ce, S.rle)}

    for k in range(K):
        h, z = T["h%d" % k], Z[k % 2]
        sa, sb = T.sem["a%d" % k], T.sem["b%d" % k]
        a.wait_ge(T.sem["u%d" % k], 1)
        a.activation(h[:, 0:512:4], z[0][:, 0:NC], relu, scale=C).then_inc(sa, 1)
        a.activation(h[:, 1:512:4], z[0][:, 0:NC], relu, scale=-C).then_inc(sa, 1)
        v.wait_ge(T.sem["v%d" % k], 1)
        v.tensor_scalar(h[:, 2:512:4], z[1][:, 0:NC], C, 0.0, AluOpType.mult, AluOpType.max).then_inc(sb, 1)
        v.tensor_scalar(h[:, 3:512:4], z[1][:, 0:NC], -C, 0.0, AluOpType.mult, AluOpType.max).then_inc(sb, 1)
        v.wait_ge(sb, 2)
        v.wait_ge(sa, 2)
        v.quantize_mx(T["hq%d" % k][:, 0:NC], T["hp%d" % k][:, 0:NC], h[:]).then_inc(T.sem["q%d" % k], 1)
        for c in outs:
            if last[c] == k - 1:
                a.wait_ge(F[c], 1)
                a.activation(STAGE[c][0][:], Y[c][:, 0:NC], copy).then_inc(STAGE[c][2], 1)

    for c in outs:
        s, t, ready, rsem = STAGE[c]
        g.wait_ge(ready, 1)
        send((s[:], t[:], c, near if c == "m" else far, rsem))

    v.wait_ge(S.fo, 1)
    acc = T.yo[:, 0:NC]
    for i, c in enumerate(outs):
        if i:
            v.wait_ge(T.sem["t%d" % i], 1)
        v.wait_ge(STAGE[c][3], nnear if c == "m" else nfar)
        out = T["acc%d" % (i + 1)][:]
        v.tensor_tensor(out, acc, STAGE[c][1][:], AluOpType.add).then_inc(T.sem["t%d" % (i + 1)], 1)
        acc = out
    g.sync.wait_ge(S.t3, 1)
    g.sync.dma_start(T.y[:], T.acc3[:]).then_inc(S.st, 16)
    g.sync.wait_ge(S.st, 16)
    g.wait_ge(S.sent, sent[0])
